import numpy as np
import ml_dtypes


def mxq(x, axis, fmt="e4m3"):
    dtype, down = {"e4m3": (ml_dtypes.float8_e4m3fn, 7), "e5m2": (ml_dtypes.float8_e5m2, 14)}[fmt]
    v = np.moveaxis(np.asarray(x, np.float32).astype(ml_dtypes.bfloat16).astype(np.float64), axis, -1)
    blocks = v.reshape(v.shape[:-1] + (-1, 32))
    amax = np.abs(blocks).max(-1, keepdims=True)
    byte = np.maximum(np.where(amax > 0, np.frexp(amax)[1] - 1 + 127, 0) - down, 1)
    scale = np.exp2(byte - 127.0)
    codes = (blocks / scale).astype(np.float32).astype(dtype).astype(np.float64)
    return np.moveaxis((codes * scale).reshape(v.shape), -1, axis)


WIDE = False


def mx_kscale(k):
    if not WIDE:
        return np.ones(k)
    levels = np.array([10, -10, 5, -5, 0])
    if k % 512:
        return np.exp2(np.random.permutation(np.resize(levels, k // 32))).repeat(32)
    a = np.empty((k // 512, 16))
    for p in range(k // 512):
        a[p, :8] = np.random.permutation(np.resize(levels, 8))
        for g in range(8):
            far = levels[np.abs(levels - a[p, g]) >= 10]
            a[p, g + 8] = far[np.random.randint(len(far))]
    return np.exp2(a.ravel()).repeat(32)


def f64(x):
    return np.asarray(x).astype(np.float64)


def striped(idx):
    return np.tile(idx.reshape(-1, 16).T, (8, 1)).astype(np.uint16)


def unstriped(offs):
    return offs[:16].T.reshape(-1).astype(np.int64)


def striped8(idx):
    return np.concatenate([x.reshape(-1, 16).T for x in idx]).astype(np.uint16)


def runs(offs, k):
    lists = np.stack([offs[16 * r : 16 * r + 16].T.reshape(-1) for r in range(8)]).astype(np.int64)
    return lists[np.arange(k) % 512 // 64]


def pack_weight(w):
    k, n = w.shape
    w = f64(np.asarray(w, np.float32).astype(ml_dtypes.bfloat16)).reshape(k // 32, 32, n)
    amax = np.abs(w).max(1)
    byte = np.clip(np.where(amax > 0, np.frexp(amax)[1] - 1 + 127 - 7, 1), 1, 254)
    scaled = (w * np.exp2(127.0 - byte)[:, None, :]).reshape(k, n).astype(np.float32)
    words = np.ascontiguousarray(scaled.reshape(k // 512, 128, 4, n).transpose(0, 1, 3, 2)).astype(ml_dtypes.float8_e4m3fn).view(np.uint8)
    return words, np.ascontiguousarray(byte.astype(np.uint8).reshape(k // 512, 16, n))


def unpack_weight(words, scales):
    g, p, n, _ = words.shape
    vals = np.ascontiguousarray(words).view(ml_dtypes.float8_e4m3fn).astype(np.float64) * np.repeat(np.exp2(scales.astype(np.float64) - 127.0), 8, axis=1)[..., None]
    return vals.transpose(0, 1, 3, 2).reshape(g * 512, n)

def planes(y):
    n, m = y.shape
    v = y.astype(np.float32).astype(ml_dtypes.bfloat16).astype(np.float64).reshape(n // 32, 32, m)
    top = np.abs(v).max(1)
    byte = np.clip(np.where(top > 0, np.frexp(top)[1] - 1 + 127 - 7, 1), 1, 254)
    codes = (v * np.exp2(127.0 - byte)[:, None, :]).reshape(n, m).astype(np.float32).astype(ml_dtypes.float8_e4m3fn).view(np.uint8)
    words = codes.reshape(n // 512, 128, 4, m).transpose(0, 1, 3, 2)
    return np.ascontiguousarray(words), np.ascontiguousarray(byte.astype(np.uint8).reshape(n // 512, 16, m))


K, T, S, V, H = 512, 2048, 512, 512, 512


def setup_inputs():
    n = np.random.standard_normal
    s = mx_kscale(K)[:, None]
    u = mx_kscale(S)
    packed_xT = pack_weight(n((K, T)) * s)
    packed_w1 = pack_weight(n((K, H)) / np.sqrt(K) / s)
    packed_w2 = pack_weight(n((K, H)) / np.sqrt(K) / s)
    packed_w3 = pack_weight(n((K, H)) / np.sqrt(K) / s)
    return {
        "x_words": packed_xT[0],
        "x_scales": packed_xT[1],
        "w1_words": packed_w1[0],
        "w1_scales": packed_w1[1],
        "w2_words": packed_w2[0],
        "w2_scales": packed_w2[1],
        "w3_words": packed_w3[0],
        "w3_scales": packed_w3[1],
        "ga": (np.random.uniform(0.5, 1.5, (H, 1)) * u[:, None]).astype(np.float32),
        "gb": (np.random.uniform(0.5, 1.5, (H, 1)) / u[:, None]).astype(np.float32),
        "offs": striped(np.random.permutation(T)[:S]),
        "two": striped(np.random.permutation(T)[:S]),
        "n1": striped8(np.stack([np.random.permutation(S) for _ in range(8)])),
        "n2": striped8(np.stack([np.random.permutation(S) for _ in range(8)])),
        "n3": striped8(np.stack([np.random.permutation(S) for _ in range(8)])),
        "three": striped(np.random.permutation(T)[:V]),
        "n4": striped8(np.stack([np.random.permutation(V) for _ in range(8)])),
        "n5": striped8(np.stack([np.random.permutation(V) for _ in range(8)])),
        "n6": striped8(np.stack([np.random.permutation(V) for _ in range(8)])),
    }


def reference(x_words, x_scales, w1_words, w1_scales, w2_words, w2_scales, w3_words, w3_scales, ga, gb, offs, two, n1, n2, n3, three, n4, n5, n6):
    xq = unpack_weight(x_words, x_scales)[:, unstriped(offs)]
    y = unpack_weight(w1_words, w1_scales).T @ xq
    x_two = unpack_weight(x_words, x_scales)[:, unstriped(two)]
    d = unpack_weight(w2_words, w2_scales).T @ x_two
    z = f64(ga) * (np.maximum(np.minimum(y - (0.5 * (y[np.arange(H)[:, None], runs(n1, H)])), d[np.arange(H)[:, None], runs(n2, H)]), d[np.arange(H)[:, None], runs(n3, H)]))
    x_three = unpack_weight(x_words, x_scales)[:, unstriped(three)]
    b = unpack_weight(w3_words, w3_scales).T @ x_three
    z2 = f64(gb) * (b / (np.abs(b[np.arange(H)[:, None], runs(n4, H)]) + 0.5))
    s = 0.0625 * ((mxq(z, 0, "e4m3").T @ mxq(z2, 0, "e4m3")))
    out_0 = s[np.arange(S)[:, None], runs(n5, S)] - (s[np.arange(S)[:, None], runs(n6, S)])
    return (out_0,) + planes(out_0)

@@ -1,0 +1,251 @@
+from contextlib import ExitStack
+
+import concourse.mybir as mybir
+
+F32 = mybir.dt.float32
+BF16 = mybir.dt.bfloat16
+I32 = mybir.dt.int32
+U32 = mybir.dt.uint32
+U16 = mybir.dt.uint16
+U8 = mybir.dt.uint8
+FP8X4 = mybir.dt.float8_e4m3fn_x4
+ALU = mybir.AluOpType
+ACT = mybir.ActivationFunctionType
+
+P = 128
+PACK = 4
+T = 2048
+N = 512
+HALF = N // 2
+OUT_PIECES = ((0, 256), (256, 128), (384, 128))
+
+FLOPS = 4 * 2 * N * N * N
+
+
+def tile_picked_twkclampbnormgap_none_po_kernel(
+    tc, x_words, x_scales, w1_words, w1_scales, w2_words, w2_scales, w3_words, w3_scales,
+    ga, gb, offs, two, n1, n2, n3, three, n4, n5, n6, out_0, out_1, out_2,
+):
+    nc = tc.nc
+    with ExitStack() as ctx:
+        lists = ctx.enter_context(tc.tile_pool(name="lists", bufs=1))
+        keep = ctx.enter_context(tc.tile_pool(name="keep", bufs=1))
+        psum = ctx.enter_context(tc.psum_pool(name="psum", bufs=8))
+
+        def load_list(name, src):
+            tile = lists.tile([P, N // 16], U16, name=name)
+            nc.sync.dma_start(tile[:], src)
+            return tile
+
+        def words_view(src):
+            return src[0].rearrange("p n t -> p (n t)").bitcast(I32)
+
+        def load_scale_rows(queue, tile, first, src):
+            for q in range(4):
+                queue.dma_start(tile[32 * q + first : 32 * q + first + 4, :].bitcast(I32), src[0, 4 * q : 4 * q + 4, :].bitcast(I32))
+
+        def entries(tile, start, width):
+            return tile[:, start // 16 : (start + width) // 16]
+
+        xw = keep.tile([P, T], U32, name="xw", align_bytes=64)
+        xs = keep.tile([P, T], U8, name="xs", align_bytes=64)
+        raw_s = keep.tile([P, N], U8, name="raw_s", tag="staged_scales", align_bytes=64)
+        raw_w = keep.tile([P, 3, N], U32, name="raw_w", tag="staged_words", align_bytes=64)
+        nc.gpsimd.memset(xs[:].bitcast(I32), 0)
+        nc.gpsimd.memset(raw_s[:].bitcast(I32), 0)
+        nc.scalar.dma_start(xw[:].bitcast(I32), words_view(x_words))
+        warm = keep.tile([P, 1], F32, name="warm")
+        warm_out = keep.tile([P, 1], F32, name="warm_out")
+        nc.vector.memset(warm[:], 1.0)
+        nc.scalar.activation(warm_out[:], warm[:], ACT.Ln)
+        offs_t = load_list("offs_t", offs)
+        two_t = load_list("two_t", two)
+        three_t = load_list("three_t", three)
+        load_scale_rows(nc.sync, xs, 0, x_scales)
+        ga_t = keep.tile([P, PACK], F32, name="ga_t")
+        gb_t = keep.tile([P, PACK], F32, name="gb_t")
+        nc.gpsimd.dma_start(ga_t[:], ga.rearrange("(p t) o -> p (t o)", t=PACK))
+        nc.gpsimd.dma_start(gb_t[:], gb.rearrange("(p t) o -> p (t o)", t=PACK))
+        load_scale_rows(nc.gpsimd, raw_s, 8, w3_scales)
+        for i, src in enumerate((w1_words, w2_words, w3_words)):
+            nc.sync.dma_start(raw_w[:, i, :].bitcast(I32), words_view(src))
+        load_scale_rows(nc.sync, raw_s, 0, w1_scales)
+        load_scale_rows(nc.sync, raw_s, 4, w2_scales)
+        n1_t = load_list("n1_t", n1)
+        n2_t = load_list("n2_t", n2)
+        n3_t = load_list("n3_t", n3)
+        n4_t = load_list("n4_t", n4)
+        n6_t = load_list("n6_t", n6)
+        n5_t = load_list("n5_t", n5)
+
+        sign = keep.tile([P, PACK], F32, name="sign")
+        step = keep.tile([P, PACK], F32, name="step")
+        ga_abs = keep.tile([P, PACK], F32, name="ga_abs")
+        ga_half = keep.tile([P, PACK], F32, name="ga_half")
+        gb_signed = keep.tile([P, PACK], F32, name="gb_signed")
+        nc.gpsimd.tensor_scalar(step[:], ga_t[:], 0.0, 2.0, ALU.is_ge, ALU.mult)
+        nc.gpsimd.tensor_scalar(sign[:], step[:], 1.0, -1.0, ALU.mult, ALU.add)
+        nc.gpsimd.tensor_tensor(ga_abs[:], ga_t[:], sign[:], ALU.mult)
+        nc.gpsimd.tensor_scalar(ga_half[:], ga_abs[:], -0.5, 0.0, ALU.mult, ALU.add)
+        nc.gpsimd.tensor_tensor(gb_signed[:], gb_t[:], sign[:], ALU.mult)
+
+        deal_s = keep.tile([P, N], U8, name="deal_s", align_bytes=64)
+        deal_w = keep.tile([P, 3, N], U32, name="deal_w", align_bytes=64)
+        pick_w, pick_s = [], []
+
+        def pick(entries_t, words_tag, scales_tag):
+            words = keep.tile([P, N], U32, name=words_tag + "_picked", tag=words_tag, align_bytes=64)
+            scales = keep.tile([P, N], U8, name=scales_tag + "_picked", tag=scales_tag, align_bytes=64)
+            nc.vector.tensor_copy(words[:], xw[:].indirect(entries_t[:]))
+            nc.vector.tensor_copy(scales[:], xs[:].indirect(entries_t[:]))
+            pick_w.append(words)
+            pick_s.append(scales)
+
+        pick(offs_t, "y_words", "y_scales")
+        pick(two_t, "d_words", "d_scales")
+        nc.vector.tensor_copy(
+            deal_w[:].bitcast(I32).rearrange("p w (t m) -> p w m t", t=PACK),
+            raw_w[:].bitcast(I32).rearrange("p w (m t) -> p w m t", t=PACK),
+        )
+        nc.vector.tensor_copy(
+            deal_s[:].rearrange("p (t m) -> p t m", t=PACK),
+            raw_s[:].rearrange("p (m t) -> p t m", t=PACK),
+        )
+        pick(three_t, "staged_words", "staged_scales")
+
+        def product(i):
+            res = []
+            for t in range(PACK):
+                bank = psum.tile([P, N], F32, name="bank")
+                cols = slice(t * P, (t + 1) * P)
+                nc.tensor.matmul_mx(
+                    out=bank[:], lhsT=deal_w[:, i, cols].bitcast(FP8X4), lhsT_scale=deal_s[4 * i :, cols],
+                    rhs=pick_w[i][:].bitcast(FP8X4), rhs_scale=pick_s[i][:], start=True, stop=True,
+                )
+                res.append(bank)
+            return res
+
+        y_ps = product(0)
+        d_ps = product(1)
+        y4 = keep.tile([P, PACK, N], F32, name="y4", align_bytes=64)
+        h_w = [keep.tile([P, N], F32, name="h_w%d" % t, align_bytes=64) for t in range(PACK)]
+        d_w = [keep.tile([P, N], F32, name="d_w%d" % t, align_bytes=64) for t in range(PACK)]
+        for t in range(PACK):
+            nc.scalar.activation(h_w[t][:], y_ps[t][:], ACT.Copy, scale=ga_half[:, t : t + 1])
+            nc.scalar.activation(y4[:, t, :], y_ps[t][:], ACT.Copy, scale=ga_abs[:, t : t + 1])
+            nc.scalar.activation(d_w[t][:], d_ps[t][:], ACT.Copy, scale=ga_abs[:, t : t + 1])
+        b_ps = product(2)
+
+        b4 = keep.tile([P, PACK, N], F32, name="b4", align_bytes=64)
+        abs4 = keep.tile([P, PACK, N], F32, name="abs4", align_bytes=64)
+        l_w = [keep.tile([P, N], F32, name="l_w%d" % t, align_bytes=64) for t in range(PACK)]
+        r_h = [keep.tile([P, PACK, HALF], F32, name="r_h%d" % u, tag="r_h%d" % u, align_bytes=64) for u in range(2)]
+        for t in range(PACK):
+            nc.scalar.activation(abs4[:, t, :], b_ps[t][:], ACT.Abs)
+            nc.scalar.activation(b4[:, t, :], b_ps[t][:], ACT.Copy, scale=gb_signed[:, t : t + 1])
+        for t in range(PACK):
+            nc.scalar.activation(l_w[t][:], abs4[:, t, :], ACT.Ln, bias=0.5)
+        for u in range(2):
+            for t in range(PACK):
+                nc.scalar.activation(r_h[u][:, t, :], l_w[t][:].indirect(entries(n4_t, u * HALF, HALF)), ACT.Exp, scale=-1.0)
+
+        a4 = keep.tile([P, PACK, N], F32, name="a4", align_bytes=64)
+        g2 = keep.tile([P, PACK, N], F32, name="g2", align_bytes=64)
+        g3 = keep.tile([P, PACK, N], F32, name="g3", align_bytes=64)
+        m4 = keep.tile([P, PACK, N], F32, name="m4", align_bytes=64)
+        for t in range(PACK):
+            for c0 in range(0, N, HALF):
+                cols = slice(c0, c0 + HALF)
+                nc.vector.tensor_tensor(a4[:, t, cols], h_w[t][:].indirect(entries(n1_t, c0, HALF)), y4[:, t, cols], ALU.add)
+            for c0 in range(0, N, HALF):
+                nc.vector.tensor_copy(g2[:, t, c0 : c0 + HALF], d_w[t][:].indirect(entries(n2_t, c0, HALF)))
+            for c0 in range(0, N, HALF):
+                nc.vector.tensor_copy(g3[:, t, c0 : c0 + HALF], d_w[t][:].indirect(entries(n3_t, c0, HALF)))
+        nc.vector.tensor_tensor(m4[:], a4[:], g2[:], ALU.min)
+
+        z2_b = [keep.tile([P, HALF * PACK], BF16, name="z2_b%d" % u, align_bytes=64) for u in range(2)]
+        z2_w = keep.tile([P, N], U32, name="z2_w", align_bytes=64)
+        z2_s = keep.tile([P, N], U8, name="z2_s", align_bytes=64)
+
+        def second_factor(u):
+            nc.vector.tensor_tensor(
+                z2_b[u][:].rearrange("p (c i t) -> p c t i", i=4, t=PACK),
+                b4[:, :, u * HALF : (u + 1) * HALF].rearrange("p t (c i) -> p c t i", i=4),
+                r_h[u][:].rearrange("p t (c i) -> p c t i", i=4),
+                ALU.mult,
+            )
+
+        def quantize_second(u):
+            cols = slice(u * HALF, (u + 1) * HALF)
+            nc.vector.quantize_mx(out=z2_w[:, cols].bitcast(FP8X4), scales=z2_s[:, cols], in_=z2_b[u][:])
+
+        z_b = []
+        z_w = [keep.tile([P, 2 * P], U32, name="z_w%d" % u, align_bytes=64) for u in range(2)]
+        z_s = [keep.tile([P, 2 * P], U8, name="z_s%d" % u, align_bytes=64) for u in range(2)]
+
+        def top(u, tag):
+            z_b.append(keep.tile([P, 2 * P * PACK], BF16, name="z_b%d" % u, tag=tag, align_bytes=64))
+            nc.vector.tensor_tensor(
+                z_b[u][:].rearrange("p (e m t) -> p m t e", e=2, t=PACK),
+                m4[:].rearrange("p t (m r) -> p m t r", r=PACK)[:, :, :, 2 * u : 2 * u + 2],
+                g3[:].rearrange("p t (m r) -> p m t r", r=PACK)[:, :, :, 2 * u : 2 * u + 2],
+                ALU.max,
+            )
+
+        s_w = [keep.tile([P, N], F32, name="s_w%d" % t, align_bytes=64) for t in range(PACK)]
+
+        def quantize_first(u):
+            nc.vector.quantize_mx(out=z_w[u][:].bitcast(FP8X4), scales=z_s[u][:], in_=z_b[u][:])
+
+        def scores(u):
+            for e in range(2):
+                bank = psum.tile([P, N], F32, name="bank")
+                cols = slice(e * P, (e + 1) * P)
+                nc.tensor.matmul_mx(
+                    out=bank[:], lhsT=z_w[u][:, cols].bitcast(FP8X4), lhsT_scale=z_s[u][:, cols],
+                    rhs=z2_w[:].bitcast(FP8X4), rhs_scale=z2_s[:], start=True, stop=True,
+                )
+                nc.scalar.activation(s_w[2 * u + e][:], bank[:], ACT.Copy, scale=0.0625)
+
+        second_factor(0)
+        top(0, "r_h0")
+        quantize_second(0)
+        second_factor(1)
+        quantize_first(0)
+        quantize_second(1)
+        scores(0)
+        top(1, "r_h1")
+        quantize_first(1)
+        scores(1)
+
+        out_rows = out_0.rearrange("(p t) v -> p t v", t=PACK)
+        out_words = out_1[0].rearrange("p n t -> p (n t)").bitcast(I32)
+        o_w = keep.tile([P, N], U32, name="o_w", align_bytes=64)
+        o_s = keep.tile([P, N], U8, name="o_s", align_bytes=64)
+
+        def finish(c0, width, o_b):
+            nc.vector.quantize_mx(out=o_w[:, c0 : c0 + width].bitcast(FP8X4), scales=o_s[:, c0 : c0 + width], in_=o_b[:])
+            nc.sync.dma_start(out_words[:, c0 : c0 + width], o_w[:, c0 : c0 + width].bitcast(I32))
+
+        waiting = None
+        for c0, width in OUT_PIECES:
+            g6 = keep.tile([P, PACK, width], F32, name="g6_%d" % c0, align_bytes=64)
+            o4 = keep.tile([P, PACK, width], F32, name="o4_%d" % c0, align_bytes=64)
+            o_b = keep.tile([P, width * PACK], BF16, name="o_b%d" % c0, align_bytes=64)
+            for t0 in range(0, PACK, 2):
+                for t in (t0, t0 + 1):
+                    nc.vector.tensor_copy(g6[:, t, :], s_w[t][:].indirect(entries(n6_t, c0, width)))
+                for t in (t0, t0 + 1):
+                    nc.vector.tensor_tensor(o4[:, t, :], s_w[t][:].indirect(entries(n5_t, c0, width)), g6[:, t, :], ALU.subtract)
+            nc.sync.dma_start(out_rows[:, :, c0 : c0 + width], o4[:])
+            nc.scalar.copy(
+                o_b[:].rearrange("p (c i t) -> p c t i", i=4, t=PACK),
+                o4[:].rearrange("p t (c i) -> p c t i", i=4),
+            )
+            if waiting is not None:
+                finish(*waiting)
+            waiting = (c0, width, o_b)
+        finish(*waiting)
+        for q in range(4):
+            queue = nc.scalar if q % 2 else nc.sync
+            queue.dma_start(out_2[0, 4 * q : 4 * q + 4, :].bitcast(I32), o_s[32 * q : 32 * q + 4, :].bitcast(I32))

@@ -53,7 +53,9 @@ def tile_picked_twkclampbnormgap_none_po_kernel(
         raw_w = keep.tile([P, 3, N], U32, name="raw_w", tag="staged_words", align_bytes=64)
         nc.gpsimd.memset(xs[:].bitcast(I32), 0)
         nc.gpsimd.memset(raw_s[:].bitcast(I32), 0)
-        nc.scalar.dma_start(xw[:].bitcast(I32), words_view(x_words))
+        h_w = [keep.tile([P, 2 * N], F32, name="h_w%d" % t, align_bytes=64) for t in range(PACK)]
+        for t in range(PACK):
+            (nc.gpsimd if t % 2 else nc.vector).memset(h_w[t][:, N:], 0.0)
         warm = keep.tile([P, 1], F32, name="warm")
         warm_out = keep.tile([P, 1], F32, name="warm_out")
         nc.vector.memset(warm[:], 1.0)
@@ -62,15 +64,15 @@ def tile_picked_twkclampbnormgap_none_po_kernel(
         two_t = load_list("two_t", two)
         three_t = load_list("three_t", three)
         load_scale_rows(nc.sync, xs, 0, x_scales)
-        ga_t = keep.tile([P, PACK], F32, name="ga_t")
-        gb_t = keep.tile([P, PACK], F32, name="gb_t")
-        nc.gpsimd.dma_start(ga_t[:], ga.rearrange("(p t) o -> p (t o)", t=PACK))
-        nc.gpsimd.dma_start(gb_t[:], gb.rearrange("(p t) o -> p (t o)", t=PACK))
-        load_scale_rows(nc.gpsimd, raw_s, 8, w3_scales)
+        nc.sync.dma_start(xw[:].bitcast(I32), words_view(x_words))
+        for i, src in enumerate((w1_scales, w2_scales, w3_scales)):
+            load_scale_rows(nc.sync, raw_s, 4 * i, src)
         for i, src in enumerate((w1_words, w2_words, w3_words)):
             nc.sync.dma_start(raw_w[:, i, :].bitcast(I32), words_view(src))
-        load_scale_rows(nc.sync, raw_s, 0, w1_scales)
-        load_scale_rows(nc.sync, raw_s, 4, w2_scales)
+        ga_t = keep.tile([P, PACK], F32, name="ga_t")
+        gb_t = keep.tile([P, PACK], F32, name="gb_t")
+        nc.sync.dma_start(ga_t[:], ga.rearrange("(p t) o -> p (t o)", t=PACK))
+        nc.sync.dma_start(gb_t[:], gb.rearrange("(p t) o -> p (t o)", t=PACK))
         n1_t = load_list("n1_t", n1)
         n2_t = load_list("n2_t", n2)
         n3_t = load_list("n3_t", n3)
@@ -78,31 +80,36 @@ def tile_picked_twkclampbnormgap_none_po_kernel(
         n6_t = load_list("n6_t", n6)
         n5_t = load_list("n5_t", n5)
 
+        sign0 = keep.tile([P, PACK], F32, name="sign0")
         sign = keep.tile([P, PACK], F32, name="sign")
-        step = keep.tile([P, PACK], F32, name="step")
         ga_abs = keep.tile([P, PACK], F32, name="ga_abs")
         ga_half = keep.tile([P, PACK], F32, name="ga_half")
         gb_signed = keep.tile([P, PACK], F32, name="gb_signed")
-        nc.gpsimd.tensor_scalar(step[:], ga_t[:], 0.0, 2.0, ALU.is_ge, ALU.mult)
-        nc.gpsimd.tensor_scalar(sign[:], step[:], 1.0, -1.0, ALU.mult, ALU.add)
-        nc.gpsimd.tensor_tensor(ga_abs[:], ga_t[:], sign[:], ALU.mult)
-        nc.gpsimd.tensor_scalar(ga_half[:], ga_abs[:], -0.5, 0.0, ALU.mult, ALU.add)
-        nc.gpsimd.tensor_tensor(gb_signed[:], gb_t[:], sign[:], ALU.mult)
+        nc.scalar.activation(ga_abs[:], ga_t[:], ACT.Abs)
+        nc.scalar.activation(sign0[:], ga_t[:], ACT.Sign)
+        nc.scalar.activation(ga_half[:], ga_abs[:], ACT.Copy, scale=-0.5)
+        nc.scalar.activation(sign[:], sign0[:], ACT.Sign, bias=0.5)
+        for t in range(PACK):
+            nc.scalar.activation(gb_signed[:, t : t + 1], gb_t[:, t : t + 1], ACT.Copy, scale=sign[:, t : t + 1])
 
         deal_s = keep.tile([P, N], U8, name="deal_s", align_bytes=64)
         deal_w = keep.tile([P, 3, N], U32, name="deal_w", align_bytes=64)
         pick_w, pick_s = [], []
 
-        def pick(entries_t, words_tag, scales_tag):
-            words = keep.tile([P, N], U32, name=words_tag + "_picked", tag=words_tag, align_bytes=64)
-            scales = keep.tile([P, N], U8, name=scales_tag + "_picked", tag=scales_tag, align_bytes=64)
-            nc.vector.tensor_copy(words[:], xw[:].indirect(entries_t[:]))
+        def pick_scales(entries_t, name):
+            scales = keep.tile([P, N], U8, name=name, align_bytes=64)
             nc.vector.tensor_copy(scales[:], xs[:].indirect(entries_t[:]))
-            pick_w.append(words)
             pick_s.append(scales)
 
-        pick(offs_t, "y_words", "y_scales")
-        pick(two_t, "d_words", "d_scales")
+        def pick_words(entries_t, name, tag):
+            words = keep.tile([P, N], U32, name=name, tag=tag, align_bytes=64)
+            nc.vector.tensor_copy(words[:], xw[:].indirect(entries_t[:]))
+            pick_w.append(words)
+
+        pick_scales(offs_t, "y_scales")
+        pick_scales(two_t, "d_scales")
+        pick_scales(three_t, "b_scales")
+        pick_words(offs_t, "y_words", "y_words")
         nc.vector.tensor_copy(
             deal_w[:].bitcast(I32).rearrange("p w (t m) -> p w m t", t=PACK),
             raw_w[:].bitcast(I32).rearrange("p w (m t) -> p w m t", t=PACK),
@@ -111,7 +118,8 @@ def tile_picked_twkclampbnormgap_none_po_kernel(
             deal_s[:].rearrange("p (t m) -> p t m", t=PACK),
             raw_s[:].rearrange("p (m t) -> p t m", t=PACK),
         )
-        pick(three_t, "staged_words", "staged_scales")
+        pick_words(two_t, "d_words", "staged_words")
+        pick_words(three_t, "b_words", "staged_scales")
 
         def product(i):
             res = []
@@ -127,13 +135,11 @@ def tile_picked_twkclampbnormgap_none_po_kernel(
 
         y_ps = product(0)
         d_ps = product(1)
-        y4 = keep.tile([P, PACK, N], F32, name="y4", align_bytes=64)
-        h_w = [keep.tile([P, N], F32, name="h_w%d" % t, align_bytes=64) for t in range(PACK)]
-        d_w = [keep.tile([P, N], F32, name="d_w%d" % t, align_bytes=64) for t in range(PACK)]
+        d_w = [keep.tile([P, 2 * N], F32, name="d_w%d" % t, align_bytes=64) for t in range(PACK)]
         for t in range(PACK):
-            nc.scalar.activation(h_w[t][:], y_ps[t][:], ACT.Copy, scale=ga_half[:, t : t + 1])
-            nc.scalar.activation(y4[:, t, :], y_ps[t][:], ACT.Copy, scale=ga_abs[:, t : t + 1])
-            nc.scalar.activation(d_w[t][:], d_ps[t][:], ACT.Copy, scale=ga_abs[:, t : t + 1])
+            nc.scalar.activation(h_w[t][:, :N], y_ps[t][:], ACT.Copy, scale=ga_half[:, t : t + 1])
+            nc.scalar.activation(d_w[t][:, N:], y_ps[t][:], ACT.Copy, scale=ga_abs[:, t : t + 1])
+            nc.scalar.activation(d_w[t][:, :N], d_ps[t][:], ACT.Copy, scale=ga_abs[:, t : t + 1])
         b_ps = product(2)
 
         b4 = keep.tile([P, PACK, N], F32, name="b4", align_bytes=64)
@@ -154,13 +160,9 @@ def tile_picked_twkclampbnormgap_none_po_kernel(
         g3 = keep.tile([P, PACK, N], F32, name="g3", align_bytes=64)
         m4 = keep.tile([P, PACK, N], F32, name="m4", align_bytes=64)
         for t in range(PACK):
-            for c0 in range(0, N, HALF):
-                cols = slice(c0, c0 + HALF)
-                nc.vector.tensor_tensor(a4[:, t, cols], h_w[t][:].indirect(entries(n1_t, c0, HALF)), y4[:, t, cols], ALU.add)
-            for c0 in range(0, N, HALF):
-                nc.vector.tensor_copy(g2[:, t, c0 : c0 + HALF], d_w[t][:].indirect(entries(n2_t, c0, HALF)))
-            for c0 in range(0, N, HALF):
-                nc.vector.tensor_copy(g3[:, t, c0 : c0 + HALF], d_w[t][:].indirect(entries(n3_t, c0, HALF)))
+            nc.vector.tensor_tensor(a4[:, t, :], h_w[t][:].indirect(n1_t[:]), d_w[t][:, N:], ALU.add)
+            nc.vector.tensor_copy(g2[:, t, :], d_w[t][:].indirect(n2_t[:]))
+            nc.vector.tensor_copy(g3[:, t, :], d_w[t][:].indirect(n3_t[:]))
         nc.vector.tensor_tensor(m4[:], a4[:], g2[:], ALU.min)
 
         z2_b = [keep.tile([P, HALF * PACK], BF16, name="z2_b%d" % u, align_bytes=64) for u in range(2)]

@@ -49,29 +49,34 @@ def tile_picked_twkclampbnormgap_none_po_kernel(
 
         xw = keep.tile([P, T], U32, name="xw", align_bytes=64)
         xs = keep.tile([P, T], U8, name="xs", align_bytes=64)
-        raw_s = keep.tile([P, N], U8, name="raw_s", tag="staged_scales", align_bytes=64)
-        raw_w = keep.tile([P, 3, N], U32, name="raw_w", tag="staged_words", align_bytes=64)
-        nc.gpsimd.memset(xs[:].bitcast(I32), 0)
-        nc.gpsimd.memset(raw_s[:].bitcast(I32), 0)
+        raw_s1 = keep.tile([P, N], U8, name="raw_s1", tag="staged_s1", align_bytes=64)
+        raw_s23 = keep.tile([P, N], U8, name="raw_s23", align_bytes=64)
+        raw_w1 = keep.tile([P, 1, N], U32, name="raw_w1", tag="staged_w1", align_bytes=64)
+        raw_w23 = keep.tile([P, 2, N], U32, name="raw_w23", tag="staged_w23", align_bytes=64)
+        nc.vector.memset(xs[:].bitcast(I32), 0)
+        nc.gpsimd.memset(raw_s1[:].bitcast(I32), 0)
+        nc.gpsimd.memset(raw_s23[:].bitcast(I32), 0)
         h_w = [keep.tile([P, 2 * N], F32, name="h_w%d" % t, align_bytes=64) for t in range(PACK)]
-        for t in range(PACK):
-            (nc.gpsimd if t % 2 else nc.vector).memset(h_w[t][:, N:], 0.0)
         warm = keep.tile([P, 1], F32, name="warm")
         warm_out = keep.tile([P, 1], F32, name="warm_out")
         nc.vector.memset(warm[:], 1.0)
         nc.scalar.activation(warm_out[:], warm[:], ACT.Ln)
+        for t in range(PACK):
+            (nc.gpsimd if t % 2 else nc.vector).memset(h_w[t][:, N:], 0.0)
         offs_t = load_list("offs_t", offs)
+        load_scale_rows(nc.sync, xs, 0, x_scales)
         two_t = load_list("two_t", two)
         three_t = load_list("three_t", three)
-        load_scale_rows(nc.sync, xs, 0, x_scales)
         nc.sync.dma_start(xw[:].bitcast(I32), words_view(x_words))
-        for i, src in enumerate((w1_scales, w2_scales, w3_scales)):
-            load_scale_rows(nc.sync, raw_s, 4 * i, src)
-        for i, src in enumerate((w1_words, w2_words, w3_words)):
-            nc.sync.dma_start(raw_w[:, i, :].bitcast(I32), words_view(src))
         ga_t = keep.tile([P, PACK], F32, name="ga_t")
         gb_t = keep.tile([P, PACK], F32, name="gb_t")
+        load_scale_rows(nc.sync, raw_s1, 0, w1_scales)
+        nc.sync.dma_start(raw_w1[:, 0, :].bitcast(I32), words_view(w1_words))
         nc.sync.dma_start(ga_t[:], ga.rearrange("(p t) o -> p (t o)", t=PACK))
+        load_scale_rows(nc.sync, raw_s23, 0, w2_scales)
+        load_scale_rows(nc.sync, raw_s23, 4, w3_scales)
+        nc.sync.dma_start(raw_w23[:, 0, :].bitcast(I32), words_view(w2_words))
+        nc.sync.dma_start(raw_w23[:, 1, :].bitcast(I32), words_view(w3_words))
         nc.sync.dma_start(gb_t[:], gb.rearrange("(p t) o -> p (t o)", t=PACK))
         n1_t = load_list("n1_t", n1)
         n2_t = load_list("n2_t", n2)
@@ -92,8 +97,22 @@ def tile_picked_twkclampbnormgap_none_po_kernel(
         for t in range(PACK):
             nc.scalar.activation(gb_signed[:, t : t + 1], gb_t[:, t : t + 1], ACT.Copy, scale=sign[:, t : t + 1])
 
-        deal_s = keep.tile([P, N], U8, name="deal_s", align_bytes=64)
-        deal_w = keep.tile([P, 3, N], U32, name="deal_w", align_bytes=64)
+        deal_s1 = keep.tile([P, N], U8, name="deal_s1", align_bytes=64)
+        deal_s23 = keep.tile([P, N], U8, name="deal_s23", align_bytes=64)
+        deal_w1 = keep.tile([P, 1, N], U32, name="deal_w1", align_bytes=64)
+        deal_w23 = keep.tile([P, 2, N], U32, name="deal_w23", align_bytes=64)
+        weights = ((deal_w1, 0, deal_s1), (deal_w23, 0, deal_s23), (deal_w23, 1, deal_s23))
+
+        def deal(words, raw_words, scales, raw_scales):
+            nc.vector.tensor_copy(
+                words[:].bitcast(I32).rearrange("p w (t m) -> p w m t", t=PACK),
+                raw_words[:].bitcast(I32).rearrange("p w (m t) -> p w m t", t=PACK),
+            )
+            nc.vector.tensor_copy(
+                scales[:].rearrange("p (t m) -> p t m", t=PACK),
+                raw_scales[:].rearrange("p (m t) -> p t m", t=PACK),
+            )
+
         pick_w, pick_s = [], []
 
         def pick_scales(entries_t, name):
@@ -110,24 +129,19 @@ def tile_picked_twkclampbnormgap_none_po_kernel(
         pick_scales(two_t, "d_scales")
         pick_scales(three_t, "b_scales")
         pick_words(offs_t, "y_words", "y_words")
-        nc.vector.tensor_copy(
-            deal_w[:].bitcast(I32).rearrange("p w (t m) -> p w m t", t=PACK),
-            raw_w[:].bitcast(I32).rearrange("p w (m t) -> p w m t", t=PACK),
-        )
-        nc.vector.tensor_copy(
-            deal_s[:].rearrange("p (t m) -> p t m", t=PACK),
-            raw_s[:].rearrange("p (m t) -> p t m", t=PACK),
-        )
-        pick_words(two_t, "d_words", "staged_words")
-        pick_words(three_t, "b_words", "staged_scales")
+        deal(deal_w1, raw_w1, deal_s1, raw_s1)
+        pick_words(two_t, "d_words", "staged_w1")
+        pick_words(three_t, "b_words", "staged_s1")
+        deal(deal_w23, raw_w23, deal_s23, raw_s23)
 
         def product(i):
             res = []
+            words, place, scales = weights[i]
             for t in range(PACK):
                 bank = psum.tile([P, N], F32, name="bank")
                 cols = slice(t * P, (t + 1) * P)
                 nc.tensor.matmul_mx(
-                    out=bank[:], lhsT=deal_w[:, i, cols].bitcast(FP8X4), lhsT_scale=deal_s[4 * i :, cols],
+                    out=bank[:], lhsT=words[:, place, cols].bitcast(FP8X4), lhsT_scale=scales[4 * place :, cols],
                     rhs=pick_w[i][:].bitcast(FP8X4), rhs_scale=pick_s[i][:], start=True, stop=True,
                 )
                 res.append(bank)
@@ -155,7 +169,7 @@ def tile_picked_twkclampbnormgap_none_po_kernel(
             for t in range(PACK):
                 nc.scalar.activation(r_h[u][:, t, :], l_w[t][:].indirect(entries(n4_t, u * HALF, HALF)), ACT.Exp, scale=-1.0)
 
-        a4 = keep.tile([P, PACK, N], F32, name="a4", align_bytes=64)
+        a4 = keep.tile([P, PACK, N], F32, name="a4", tag="staged_w23", align_bytes=64)
         g2 = keep.tile([P, PACK, N], F32, name="g2", align_bytes=64)
         g3 = keep.tile([P, PACK, N], F32, name="g3", align_bytes=64)
         m4 = keep.tile([P, PACK, N], F32, name="m4", align_bytes=64)
@@ -194,7 +208,7 @@ def tile_picked_twkclampbnormgap_none_po_kernel(
                 ALU.max,
             )
 
-        s_w = [keep.tile([P, N], F32, name="s_w%d" % t, align_bytes=64) for t in range(PACK)]
+        s_w = h_w[: PACK - 1] + [keep.tile([P, N], F32, name="s_last", align_bytes=64)]
 
         def quantize_first(u):
             nc.vector.quantize_mx(out=z_w[u][:].bitcast(FP8X4), scales=z_s[u][:], in_=z_b[u][:])
@@ -207,7 +221,7 @@ def tile_picked_twkclampbnormgap_none_po_kernel(
                     out=bank[:], lhsT=z_w[u][:, cols].bitcast(FP8X4), lhsT_scale=z_s[u][:, cols],
                     rhs=z2_w[:].bitcast(FP8X4), rhs_scale=z2_s[:], start=True, stop=True,
                 )
-                nc.scalar.activation(s_w[2 * u + e][:], bank[:], ACT.Copy, scale=0.0625)
+                nc.scalar.activation(s_w[2 * u + e][:, :N], bank[:], ACT.Copy, scale=0.0625)
 
         second_factor(0)
         top(0, "r_h0")
@@ -229,25 +243,43 @@ def tile_picked_twkclampbnormgap_none_po_kernel(
             nc.vector.quantize_mx(out=o_w[:, c0 : c0 + width].bitcast(FP8X4), scales=o_s[:, c0 : c0 + width], in_=o_b[:])
             nc.sync.dma_start(out_words[:, c0 : c0 + width], o_w[:, c0 : c0 + width].bitcast(I32))
 
-        waiting = None
-        for c0, width in OUT_PIECES:
-            g6 = keep.tile([P, PACK, width], F32, name="g6_%d" % c0, align_bytes=64)
-            o4 = keep.tile([P, PACK, width], F32, name="o4_%d" % c0, align_bytes=64)
-            o_b = keep.tile([P, width * PACK], BF16, name="o_b%d" % c0, align_bytes=64)
-            for t0 in range(0, PACK, 2):
-                for t in (t0, t0 + 1):
-                    nc.vector.tensor_copy(g6[:, t, :], s_w[t][:].indirect(entries(n6_t, c0, width)))
-                for t in (t0, t0 + 1):
-                    nc.vector.tensor_tensor(o4[:, t, :], s_w[t][:].indirect(entries(n5_t, c0, width)), g6[:, t, :], ALU.subtract)
-            nc.sync.dma_start(out_rows[:, :, c0 : c0 + width], o4[:])
+        g6 = keep.tile([P, PACK, N], F32, name="g6", align_bytes=64)
+        o4 = keep.tile([P, PACK, N], F32, name="o4", align_bytes=64)
+
+        def fetch(t, c0, width):
+            nc.vector.tensor_copy(g6[:, t, c0 : c0 + width], s_w[t][:].indirect(entries(n6_t, c0, width)))
+
+        def gap(t, c0, width):
+            cols = slice(c0, c0 + width)
+            nc.vector.tensor_tensor(o4[:, t, cols], s_w[t][:].indirect(entries(n5_t, c0, width)), g6[:, t, cols], ALU.subtract)
+            nc.sync.dma_start(out_rows[:, t, cols], o4[:, t, cols])
+
+        def round_pair(first, c0, width, o_b):
             nc.scalar.copy(
-                o_b[:].rearrange("p (c i t) -> p c t i", i=4, t=PACK),
-                o4[:].rearrange("p t (c i) -> p c t i", i=4),
+                o_b[:].rearrange("p (c t) -> p c t", t=PACK)[:, :, first : first + 2],
+                o4[:, first : first + 2, c0 : c0 + width].rearrange("p t c -> p c t"),
             )
-            if waiting is not None:
-                finish(*waiting)
-            waiting = (c0, width, o_b)
-        finish(*waiting)
+
+        rounded = [
+            (c0, width, keep.tile([P, width * PACK], BF16, name="o_b%d" % c0, align_bytes=64))
+            for c0, width in OUT_PIECES
+        ]
+        last = PACK - 1
+        fetch(0, 0, N)
+        fetch(1, 0, N)
+        gap(0, 0, N)
+        gap(1, 0, N)
+        for piece in rounded:
+            round_pair(0, *piece)
+        fetch(2, 0, N)
+        fetch(last, 0, HALF)
+        fetch(last, HALF, HALF)
+        gap(2, 0, N)
+        for piece in rounded:
+            gap(last, piece[0], piece[1])
+            round_pair(2, *piece)
+        for piece in rounded:
+            finish(*piece)
         for q in range(4):
             queue = nc.scalar if q % 2 else nc.sync
             queue.dma_start(out_2[0, 4 * q : 4 * q + 4, :].bitcast(I32), o_s[32 * q : 32 * q + 4, :].bitcast(I32))

@@ -105,34 +105,25 @@ def tile_picked_twkclampbnormgap_none_po_kernel(
 
         def deal(words, raw_words, scales, raw_scales):
             nc.vector.tensor_copy(
-                words[:].bitcast(I32).rearrange("p w (t m) -> p w m t", t=PACK),
-                raw_words[:].bitcast(I32).rearrange("p w (m t) -> p w m t", t=PACK),
+                words[:].bitcast(I32).rearrange("p w (t c i) -> p w c t i", t=PACK, i=4),
+                raw_words[:].bitcast(I32).rearrange("p w (c i t) -> p w c t i", t=PACK, i=4),
             )
             nc.vector.tensor_copy(
                 scales[:].rearrange("p (t m) -> p t m", t=PACK),
                 raw_scales[:].rearrange("p (m t) -> p t m", t=PACK),
             )
 
-        pick_w, pick_s = [], []
+        pick_w, pick_s = {}, {}
 
-        def pick_scales(entries_t, name):
-            scales = keep.tile([P, N], U8, name=name, align_bytes=64)
+        def pick_scales(i, entries_t, tag):
+            scales = keep.tile([P, N], U8, name="pick_s%d" % i, tag=tag, align_bytes=64)
             nc.vector.tensor_copy(scales[:], xs[:].indirect(entries_t[:]))
-            pick_s.append(scales)
+            pick_s[i] = scales
 
-        def pick_words(entries_t, name, tag):
-            words = keep.tile([P, N], U32, name=name, tag=tag, align_bytes=64)
+        def pick_words(i, entries_t, tag):
+            words = keep.tile([P, N], U32, name="pick_w%d" % i, tag=tag, align_bytes=64)
             nc.vector.tensor_copy(words[:], xw[:].indirect(entries_t[:]))
-            pick_w.append(words)
-
-        pick_scales(offs_t, "y_scales")
-        pick_scales(two_t, "d_scales")
-        pick_scales(three_t, "b_scales")
-        pick_words(offs_t, "y_words", "y_words")
-        deal(deal_w1, raw_w1, deal_s1, raw_s1)
-        pick_words(two_t, "d_words", "staged_w1")
-        pick_words(three_t, "b_words", "staged_s1")
-        deal(deal_w23, raw_w23, deal_s23, raw_s23)
+            pick_w[i] = words
 
         def product(i):
             res = []
@@ -147,7 +138,15 @@ def tile_picked_twkclampbnormgap_none_po_kernel(
                 res.append(bank)
             return res
 
+        pick_scales(0, offs_t, "y_scales")
+        pick_scales(1, two_t, "d_scales")
+        pick_words(0, offs_t, "y_words")
+        deal(deal_w1, raw_w1, deal_s1, raw_s1)
         y_ps = product(0)
+        pick_words(1, two_t, "staged_w1")
+        pick_scales(2, three_t, "staged_s1")
+        pick_words(2, three_t, "y_words")
+        deal(deal_w23, raw_w23, deal_s23, raw_s23)
         d_ps = product(1)
         d_w = [keep.tile([P, 2 * N], F32, name="d_w%d" % t, align_bytes=64) for t in range(PACK)]
         for t in range(PACK):
@@ -172,12 +171,10 @@ def tile_picked_twkclampbnormgap_none_po_kernel(
         a4 = keep.tile([P, PACK, N], F32, name="a4", tag="staged_w23", align_bytes=64)
         g2 = keep.tile([P, PACK, N], F32, name="g2", align_bytes=64)
         g3 = keep.tile([P, PACK, N], F32, name="g3", align_bytes=64)
-        m4 = keep.tile([P, PACK, N], F32, name="m4", align_bytes=64)
         for t in range(PACK):
             nc.vector.tensor_tensor(a4[:, t, :], h_w[t][:].indirect(n1_t[:]), d_w[t][:, N:], ALU.add)
             nc.vector.tensor_copy(g2[:, t, :], d_w[t][:].indirect(n2_t[:]))
             nc.vector.tensor_copy(g3[:, t, :], d_w[t][:].indirect(n3_t[:]))
-        nc.vector.tensor_tensor(m4[:], a4[:], g2[:], ALU.min)
 
         z2_b = [keep.tile([P, HALF * PACK], BF16, name="z2_b%d" % u, align_bytes=64) for u in range(2)]
         z2_w = keep.tile([P, N], U32, name="z2_w", align_bytes=64)
@@ -185,9 +182,9 @@ def tile_picked_twkclampbnormgap_none_po_kernel(
 
         def second_factor(u):
             nc.vector.tensor_tensor(
-                z2_b[u][:].rearrange("p (c i t) -> p c t i", i=4, t=PACK),
-                b4[:, :, u * HALF : (u + 1) * HALF].rearrange("p t (c i) -> p c t i", i=4),
-                r_h[u][:].rearrange("p t (c i) -> p c t i", i=4),
+                z2_b[u][:].rearrange("p (c i t) -> p c t i", i=2, t=PACK),
+                b4[:, :, u * HALF : (u + 1) * HALF].rearrange("p t (c i) -> p c t i", i=2),
+                r_h[u][:].rearrange("p t (c i) -> p c t i", i=2),
                 ALU.mult,
             )
 
@@ -196,17 +193,26 @@ def tile_picked_twkclampbnormgap_none_po_kernel(
             nc.vector.quantize_mx(out=z2_w[:, cols].bitcast(FP8X4), scales=z2_s[:, cols], in_=z2_b[u][:])
 
         z_b = []
+        low = []
         z_w = [keep.tile([P, 2 * P], U32, name="z_w%d" % u, align_bytes=64) for u in range(2)]
         z_s = [keep.tile([P, 2 * P], U8, name="z_s%d" % u, align_bytes=64) for u in range(2)]
 
-        def top(u, tag):
-            z_b.append(keep.tile([P, 2 * P * PACK], BF16, name="z_b%d" % u, tag=tag, align_bytes=64))
-            nc.vector.tensor_tensor(
-                z_b[u][:].rearrange("p (e m t) -> p m t e", e=2, t=PACK),
-                m4[:].rearrange("p t (m r) -> p m t r", r=PACK)[:, :, :, 2 * u : 2 * u + 2],
-                g3[:].rearrange("p t (m r) -> p m t r", r=PACK)[:, :, :, 2 * u : 2 * u + 2],
-                ALU.max,
-            )
+        def pairs(planes, u):
+            return planes[:].rearrange("p t (m r) -> p t m r", r=PACK)[:, :, :, 2 * u : 2 * u + 2]
+
+        def smaller(u, tag):
+            low.append(keep.tile([P, PACK, P, 2], F32, name="low%d" % u, tag=tag, align_bytes=64))
+            nc.vector.tensor_tensor(low[u][:], pairs(a4, u), pairs(g2, u), ALU.min)
+
+        def larger(u, tag, woven_tag):
+            z_p = keep.tile([P, PACK, P, 2], BF16, name="z_p%d" % u, tag=tag, align_bytes=64)
+            z_b.append(keep.tile([P, 2 * P * PACK], BF16, name="z_b%d" % u, tag=woven_tag, align_bytes=64))
+            nc.vector.tensor_tensor(z_p[:], low[u][:], pairs(g3, u), ALU.max)
+
+            def weave():
+                nc.scalar.copy(z_b[u][:].rearrange("p (e m t) -> p e m t", e=2, t=PACK), z_p[:].rearrange("p t m e -> p e m t"))
+
+            return weave
 
         s_w = h_w[: PACK - 1] + [keep.tile([P, N], F32, name="s_last", align_bytes=64)]
 
@@ -223,14 +229,17 @@ def tile_picked_twkclampbnormgap_none_po_kernel(
                 )
                 nc.scalar.activation(s_w[2 * u + e][:, :N], bank[:], ACT.Copy, scale=0.0625)
 
+        smaller(0, "low0")
+        larger(0, "z_p0", "z_b0")()
         second_factor(0)
-        top(0, "r_h0")
+        smaller(1, "r_h0")
         quantize_second(0)
-        second_factor(1)
         quantize_first(0)
+        second_factor(1)
         quantize_second(1)
+        weave_last = larger(1, "r_h1", "z_b1")
         scores(0)
-        top(1, "r_h1")
+        weave_last()
         quantize_first(1)
         scores(1)
 
@@ -244,7 +253,7 @@ def tile_picked_twkclampbnormgap_none_po_kernel(
             nc.sync.dma_start(out_words[:, c0 : c0 + width], o_w[:, c0 : c0 + width].bitcast(I32))
 
         g6 = keep.tile([P, PACK, N], F32, name="g6", align_bytes=64)
-        o4 = keep.tile([P, PACK, N], F32, name="o4", align_bytes=64)
+        o4 = keep.tile([P, PACK, N], F32, name="o4", tag="z_b1", align_bytes=64)
 
         def fetch(t, c0, width):
             nc.vector.tensor_copy(g6[:, t, c0 : c0 + width], s_w[t][:].indirect(entries(n6_t, c0, width)))

@@ -120,9 +120,8 @@ def tile_picked_twkclampbnormgap_none_po_kernel(
             nc.vector.tensor_copy(scales[:], xs[:].indirect(entries_t[:]))
             pick_s[i] = scales
 
-        def pick_words(i, entries_t, tag):
-            words = keep.tile([P, N], U32, name="pick_w%d" % i, tag=tag, align_bytes=64)
-            nc.vector.tensor_copy(words[:], xw[:].indirect(entries_t[:]))
+        def pick_words(i, entries_t, words):
+            nc.vector.tensor_copy(words, xw[:].indirect(entries_t[:]))
             pick_w[i] = words
 
         def product(i):
@@ -133,19 +132,21 @@ def tile_picked_twkclampbnormgap_none_po_kernel(
                 cols = slice(t * P, (t + 1) * P)
                 nc.tensor.matmul_mx(
                     out=bank[:], lhsT=words[:, place, cols].bitcast(FP8X4), lhsT_scale=scales[4 * place :, cols],
-                    rhs=pick_w[i][:].bitcast(FP8X4), rhs_scale=pick_s[i][:], start=True, stop=True,
+                    rhs=pick_w[i].bitcast(FP8X4), rhs_scale=pick_s[i][:], start=True, stop=True,
                 )
                 res.append(bank)
             return res
 
         pick_scales(0, offs_t, "y_scales")
         pick_scales(1, two_t, "d_scales")
-        pick_words(0, offs_t, "y_words")
+        y_words = keep.tile([P, N], U32, name="y_words", align_bytes=64)
+        pick_words(0, offs_t, y_words[:])
         deal(deal_w1, raw_w1, deal_s1, raw_s1)
         y_ps = product(0)
-        pick_words(1, two_t, "staged_w1")
+        db_words = keep.tile([P, 2, N], U32, name="db_words", tag="staged_w1", align_bytes=64)
+        pick_words(1, two_t, db_words[:, 0, :])
+        pick_words(2, three_t, db_words[:, 1, :])
         pick_scales(2, three_t, "staged_s1")
-        pick_words(2, three_t, "y_words")
         deal(deal_w23, raw_w23, deal_s23, raw_s23)
         d_ps = product(1)
         d_w = [keep.tile([P, 2 * N], F32, name="d_w%d" % t, align_bytes=64) for t in range(PACK)]
@@ -156,92 +157,68 @@ def tile_picked_twkclampbnormgap_none_po_kernel(
         b_ps = product(2)
 
         b4 = keep.tile([P, PACK, N], F32, name="b4", align_bytes=64)
-        abs4 = keep.tile([P, PACK, N], F32, name="abs4", align_bytes=64)
-        l_w = [keep.tile([P, N], F32, name="l_w%d" % t, align_bytes=64) for t in range(PACK)]
-        r_h = [keep.tile([P, PACK, HALF], F32, name="r_h%d" % u, tag="r_h%d" % u, align_bytes=64) for u in range(2)]
+        l_w = [keep.tile([P, 2 * N], F32, name="l_w%d" % t, align_bytes=64) for t in range(PACK)]
+        r4 = keep.tile([P, PACK, N], F32, name="r4", align_bytes=64)
         for t in range(PACK):
-            nc.scalar.activation(abs4[:, t, :], b_ps[t][:], ACT.Abs)
+            nc.scalar.activation(l_w[t][:, N:], b_ps[t][:], ACT.Abs)
             nc.scalar.activation(b4[:, t, :], b_ps[t][:], ACT.Copy, scale=gb_signed[:, t : t + 1])
         for t in range(PACK):
-            nc.scalar.activation(l_w[t][:], abs4[:, t, :], ACT.Ln, bias=0.5)
-        for u in range(2):
-            for t in range(PACK):
-                nc.scalar.activation(r_h[u][:, t, :], l_w[t][:].indirect(entries(n4_t, u * HALF, HALF)), ACT.Exp, scale=-1.0)
+            nc.scalar.activation(l_w[t][:, :N], l_w[t][:, N:], ACT.Ln, bias=0.5)
+        for t in range(PACK):
+            nc.scalar.activation(r4[:, t, :], l_w[t][:].indirect(n4_t[:]), ACT.Exp, scale=-1.0)
 
         a4 = keep.tile([P, PACK, N], F32, name="a4", tag="staged_w23", align_bytes=64)
         g2 = keep.tile([P, PACK, N], F32, name="g2", align_bytes=64)
-        g3 = keep.tile([P, PACK, N], F32, name="g3", align_bytes=64)
+        g3 = keep.tile([P, PACK, N], BF16, name="g3", align_bytes=64)
         for t in range(PACK):
             nc.vector.tensor_tensor(a4[:, t, :], h_w[t][:].indirect(n1_t[:]), d_w[t][:, N:], ALU.add)
             nc.vector.tensor_copy(g2[:, t, :], d_w[t][:].indirect(n2_t[:]))
             nc.vector.tensor_copy(g3[:, t, :], d_w[t][:].indirect(n3_t[:]))
 
-        z2_b = [keep.tile([P, HALF * PACK], BF16, name="z2_b%d" % u, align_bytes=64) for u in range(2)]
+        low = keep.tile([P, PACK, N], BF16, name="low", align_bytes=64)
+        z_p = keep.tile([P, PACK, N], BF16, name="z_p", align_bytes=64)
+        nc.vector.tensor_tensor(low[:], a4[:], g2[:], ALU.min)
+        nc.vector.tensor_tensor(z_p[:], low[:], g3[:], ALU.max)
+        z_b = [keep.tile([P, 2 * P * PACK], BF16, name="z_b%d" % u, align_bytes=64) for u in range(2)]
+        for u in range(2):
+            nc.scalar.copy(
+                z_b[u][:].rearrange("p (e m t) -> p e m t", e=2, t=PACK),
+                z_p[:].rearrange("p t (m r) -> p r m t", r=PACK)[:, 2 * u : 2 * u + 2],
+            )
+        z2_b = keep.tile([P, N * PACK], BF16, name="z2_b", align_bytes=64)
         z2_w = keep.tile([P, N], U32, name="z2_w", align_bytes=64)
         z2_s = keep.tile([P, N], U8, name="z2_s", align_bytes=64)
-
-        def second_factor(u):
-            nc.vector.tensor_tensor(
-                z2_b[u][:].rearrange("p (c i t) -> p c t i", i=2, t=PACK),
-                b4[:, :, u * HALF : (u + 1) * HALF].rearrange("p t (c i) -> p c t i", i=2),
-                r_h[u][:].rearrange("p t (c i) -> p c t i", i=2),
-                ALU.mult,
-            )
-
-        def quantize_second(u):
-            cols = slice(u * HALF, (u + 1) * HALF)
-            nc.vector.quantize_mx(out=z2_w[:, cols].bitcast(FP8X4), scales=z2_s[:, cols], in_=z2_b[u][:])
-
-        z_b = []
-        low = []
+        nc.vector.tensor_tensor(
+            z2_b[:].rearrange("p (c i t) -> p c t i", i=2, t=PACK),
+            b4[:].rearrange("p t (c i) -> p c t i", i=2),
+            r4[:].rearrange("p t (c i) -> p c t i", i=2),
+            ALU.mult,
+        )
         z_w = [keep.tile([P, 2 * P], U32, name="z_w%d" % u, align_bytes=64) for u in range(2)]
         z_s = [keep.tile([P, 2 * P], U8, name="z_s%d" % u, align_bytes=64) for u in range(2)]
-
-        def pairs(planes, u):
-            return planes[:].rearrange("p t (m r) -> p t m r", r=PACK)[:, :, :, 2 * u : 2 * u + 2]
-
-        def smaller(u, tag):
-            low.append(keep.tile([P, PACK, P, 2], F32, name="low%d" % u, tag=tag, align_bytes=64))
-            nc.vector.tensor_tensor(low[u][:], pairs(a4, u), pairs(g2, u), ALU.min)
-
-        def larger(u, tag, woven_tag):
-            z_p = keep.tile([P, PACK, P, 2], BF16, name="z_p%d" % u, tag=tag, align_bytes=64)
-            z_b.append(keep.tile([P, 2 * P * PACK], BF16, name="z_b%d" % u, tag=woven_tag, align_bytes=64))
-            nc.vector.tensor_tensor(z_p[:], low[u][:], pairs(g3, u), ALU.max)
-
-            def weave():
-                nc.scalar.copy(z_b[u][:].rearrange("p (e m t) -> p e m t", e=2, t=PACK), z_p[:].rearrange("p t m e -> p e m t"))
-
-            return weave
 
         s_w = h_w[: PACK - 1] + [keep.tile([P, N], F32, name="s_last", align_bytes=64)]
 
         def quantize_first(u):
             nc.vector.quantize_mx(out=z_w[u][:].bitcast(FP8X4), scales=z_s[u][:], in_=z_b[u][:])
 
-        def scores(u):
-            for e in range(2):
-                bank = psum.tile([P, N], F32, name="bank")
-                cols = slice(e * P, (e + 1) * P)
-                nc.tensor.matmul_mx(
-                    out=bank[:], lhsT=z_w[u][:, cols].bitcast(FP8X4), lhsT_scale=z_s[u][:, cols],
-                    rhs=z2_w[:].bitcast(FP8X4), rhs_scale=z2_s[:], start=True, stop=True,
-                )
-                nc.scalar.activation(s_w[2 * u + e][:, :N], bank[:], ACT.Copy, scale=0.0625)
+        def score_bank(t, c0, width):
+            bank = psum.tile([P, width], F32, name="bank")
+            rows = slice(t % 2 * P, (t % 2 + 1) * P)
+            nc.tensor.matmul_mx(
+                out=bank[:], lhsT=z_w[t // 2][:, rows].bitcast(FP8X4), lhsT_scale=z_s[t // 2][:, rows],
+                rhs=z2_w[:, c0 : c0 + width].bitcast(FP8X4), rhs_scale=z2_s[:, c0 : c0 + width], start=True, stop=True,
+            )
+            return bank
 
-        smaller(0, "low0")
-        larger(0, "z_p0", "z_b0")()
-        second_factor(0)
-        smaller(1, "r_h0")
-        quantize_second(0)
         quantize_first(0)
-        second_factor(1)
-        quantize_second(1)
-        weave_last = larger(1, "r_h1", "z_b1")
-        scores(0)
-        weave_last()
+        nc.vector.quantize_mx(out=z2_w[:].bitcast(FP8X4), scales=z2_s[:], in_=z2_b[:])
         quantize_first(1)
-        scores(1)
+        left, right = score_bank(0, 0, HALF), score_bank(0, HALF, HALF)
+        nc.scalar.activation(s_w[0][:, :HALF], left[:], ACT.Copy, scale=0.0625)
+        nc.vector.tensor_scalar(s_w[0][:, HALF:N], right[:], 0.0625, None, ALU.mult)
+        for t in range(1, PACK):
+            nc.scalar.activation(s_w[t][:, :N], score_bank(t, 0, N)[:], ACT.Copy, scale=0.0625)
 
         out_rows = out_0.rearrange("(p t) v -> p t v", t=PACK)
         out_words = out_1[0].rearrange("p n t -> p (n t)").bitcast(I32)
@@ -253,7 +230,7 @@ def tile_picked_twkclampbnormgap_none_po_kernel(
             nc.sync.dma_start(out_words[:, c0 : c0 + width], o_w[:, c0 : c0 + width].bitcast(I32))
 
         g6 = keep.tile([P, PACK, N], F32, name="g6", align_bytes=64)
-        o4 = keep.tile([P, PACK, N], F32, name="o4", tag="z_b1", align_bytes=64)
+        o4 = keep.tile([P, PACK, N], F32, name="o4", align_bytes=64)
 
         def fetch(t, c0, width):
             nc.vector.tensor_copy(g6[:, t, c0 : c0 + width], s_w[t][:].indirect(entries(n6_t, c0, width)))
@@ -263,8 +240,8 @@ def tile_picked_twkclampbnormgap_none_po_kernel(
             nc.vector.tensor_tensor(o4[:, t, cols], s_w[t][:].indirect(entries(n5_t, c0, width)), g6[:, t, cols], ALU.subtract)
             nc.sync.dma_start(out_rows[:, t, cols], o4[:, t, cols])
 
-        def round_pair(first, c0, width, o_b):
-            nc.scalar.copy(
+        def round_pair(copy, first, c0, width, o_b):
+            copy(
                 o_b[:].rearrange("p (c t) -> p c t", t=PACK)[:, :, first : first + 2],
                 o4[:, first : first + 2, c0 : c0 + width].rearrange("p t c -> p c t"),
             )
@@ -279,14 +256,14 @@ def tile_picked_twkclampbnormgap_none_po_kernel(
         gap(0, 0, N)
         gap(1, 0, N)
         for piece in rounded:
-            round_pair(0, *piece)
+            round_pair(nc.scalar.copy, 0, *piece)
         fetch(2, 0, N)
         fetch(last, 0, HALF)
         fetch(last, HALF, HALF)
         gap(2, 0, N)
         for piece in rounded:
             gap(last, piece[0], piece[1])
-            round_pair(2, *piece)
+            round_pair(nc.vector.tensor_copy if piece[0] == OUT_PIECES[-1][0] else nc.scalar.copy, 2, *piece)
         for piece in rounded:
             finish(*piece)
         for q in range(4):

from contextlib import ExitStack

import concourse.mybir as mybir

F32 = mybir.dt.float32
BF16 = mybir.dt.bfloat16
I32 = mybir.dt.int32
U32 = mybir.dt.uint32
U16 = mybir.dt.uint16
U8 = mybir.dt.uint8
FP8X4 = mybir.dt.float8_e4m3fn_x4
ALU = mybir.AluOpType
ACT = mybir.ActivationFunctionType

P = 128
PACK = 4
T = 2048
N = 512
HALF = N // 2
OUT_PIECES = ((0, 256), (256, 128), (384, 128))

FLOPS = 4 * 2 * N * N * N


def tile_picked_twkclampbnormgap_none_po_kernel(
    tc, x_words, x_scales, w1_words, w1_scales, w2_words, w2_scales, w3_words, w3_scales,
    ga, gb, offs, two, n1, n2, n3, three, n4, n5, n6, out_0, out_1, out_2,
):
    nc = tc.nc
    with ExitStack() as ctx:
        lists = ctx.enter_context(tc.tile_pool(name="lists", bufs=1))
        keep = ctx.enter_context(tc.tile_pool(name="keep", bufs=1))
        psum = ctx.enter_context(tc.psum_pool(name="psum", bufs=8))

        def load_list(name, src):
            tile = lists.tile([P, N // 16], U16, name=name)
            nc.sync.dma_start(tile[:], src)
            return tile

        def words_view(src):
            return src[0].rearrange("p n t -> p (n t)").bitcast(I32)

        def load_scale_rows(queue, tile, first, src):
            for q in range(4):
                queue.dma_start(tile[32 * q + first : 32 * q + first + 4, :].bitcast(I32), src[0, 4 * q : 4 * q + 4, :].bitcast(I32))

        def entries(tile, start, width):
            return tile[:, start // 16 : (start + width) // 16]

        xw = keep.tile([P, T], U32, name="xw", align_bytes=64)
        xs = keep.tile([P, T], U8, name="xs", align_bytes=64)
        raw_s1 = keep.tile([P, N], U8, name="raw_s1", tag="staged_s1", align_bytes=64)
        raw_s23 = keep.tile([P, N], U8, name="raw_s23", align_bytes=64)
        raw_w1 = keep.tile([P, 1, N], U32, name="raw_w1", tag="staged_w1", align_bytes=64)
        raw_w23 = keep.tile([P, 2, N], U32, name="raw_w23", tag="staged_w23", align_bytes=64)
        nc.vector.memset(xs[:].bitcast(I32), 0)
        nc.gpsimd.memset(raw_s1[:].bitcast(I32), 0)
        nc.gpsimd.memset(raw_s23[:].bitcast(I32), 0)
        h_w = [keep.tile([P, 2 * N], F32, name="h_w%d" % t, align_bytes=64) for t in range(PACK)]
        warm = keep.tile([P, 1], F32, name="warm")
        warm_out = keep.tile([P, 1], F32, name="warm_out")
        nc.vector.memset(warm[:], 1.0)
        nc.scalar.activation(warm_out[:], warm[:], ACT.Ln)
        for t in range(PACK):
            (nc.gpsimd if t % 2 else nc.vector).memset(h_w[t][:, N:], 0.0)
        offs_t = load_list("offs_t", offs)
        load_scale_rows(nc.sync, xs, 0, x_scales)
        two_t = load_list("two_t", two)
        three_t = load_list("three_t", three)
        nc.sync.dma_start(xw[:].bitcast(I32), words_view(x_words))
        ga_t = keep.tile([P, PACK], F32, name="ga_t")
        gb_t = keep.tile([P, PACK], F32, name="gb_t")
        load_scale_rows(nc.sync, raw_s1, 0, w1_scales)
        nc.sync.dma_start(raw_w1[:, 0, :].bitcast(I32), words_view(w1_words))
        nc.sync.dma_start(ga_t[:], ga.rearrange("(p t) o -> p (t o)", t=PACK))
        load_scale_rows(nc.sync, raw_s23, 0, w2_scales)
        load_scale_rows(nc.sync, raw_s23, 4, w3_scales)
        nc.sync.dma_start(raw_w23[:, 0, :].bitcast(I32), words_view(w2_words))
        nc.sync.dma_start(raw_w23[:, 1, :].bitcast(I32), words_view(w3_words))
        nc.sync.dma_start(gb_t[:], gb.rearrange("(p t) o -> p (t o)", t=PACK))
        n1_t = load_list("n1_t", n1)
        n2_t = load_list("n2_t", n2)
        n3_t = load_list("n3_t", n3)
        n4_t = load_list("n4_t", n4)
        n6_t = load_list("n6_t", n6)
        n5_t = load_list("n5_t", n5)

        sign0 = keep.tile([P, PACK], F32, name="sign0")
        sign = keep.tile([P, PACK], F32, name="sign")
        ga_abs = keep.tile([P, PACK], F32, name="ga_abs")
        ga_half = keep.tile([P, PACK], F32, name="ga_half")
        gb_signed = keep.tile([P, PACK], F32, name="gb_signed")
        nc.scalar.activation(ga_abs[:], ga_t[:], ACT.Abs)
        nc.scalar.activation(sign0[:], ga_t[:], ACT.Sign)
        nc.scalar.activation(ga_half[:], ga_abs[:], ACT.Copy, scale=-0.5)
        nc.scalar.activation(sign[:], sign0[:], ACT.Sign, bias=0.5)
        for t in range(PACK):
            nc.scalar.activation(gb_signed[:, t : t + 1], gb_t[:, t : t + 1], ACT.Copy, scale=sign[:, t : t + 1])

        deal_s1 = keep.tile([P, N], U8, name="deal_s1", align_bytes=64)
        deal_s23 = keep.tile([P, N], U8, name="deal_s23", align_bytes=64)
        deal_w1 = keep.tile([P, 1, N], U32, name="deal_w1", align_bytes=64)
        deal_w23 = keep.tile([P, 2, N], U32, name="deal_w23", align_bytes=64)
        weights = ((deal_w1, 0, deal_s1), (deal_w23, 0, deal_s23), (deal_w23, 1, deal_s23))

        def deal(words, raw_words, scales, raw_scales):
            nc.vector.tensor_copy(
                words[:].bitcast(I32).rearrange("p w (t c i) -> p w c t i", t=PACK, i=4),
                raw_words[:].bitcast(I32).rearrange("p w (c i t) -> p w c t i", t=PACK, i=4),
            )
            nc.vector.tensor_copy(
                scales[:].rearrange("p (t m) -> p t m", t=PACK),
                raw_scales[:].rearrange("p (m t) -> p t m", t=PACK),
            )

        pick_w, pick_s = {}, {}

        def pick_scales(i, entries_t, tag):
            scales = keep.tile([P, N], U8, name="pick_s%d" % i, tag=tag, align_bytes=64)
            nc.vector.tensor_copy(scales[:], xs[:].indirect(entries_t[:]))
            pick_s[i] = scales

        def pick_words(i, entries_t, words):
            nc.vector.tensor_copy(words, xw[:].indirect(entries_t[:]))
            pick_w[i] = words

        def product(i):
            res = []
            words, place, scales = weights[i]
            for t in range(PACK):
                bank = psum.tile([P, N], F32, name="bank")
                cols = slice(t * P, (t + 1) * P)
                nc.tensor.matmul_mx(
                    out=bank[:], lhsT=words[:, place, cols].bitcast(FP8X4), lhsT_scale=scales[4 * place :, cols],
                    rhs=pick_w[i].bitcast(FP8X4), rhs_scale=pick_s[i][:], start=True, stop=True,
                )
                res.append(bank)
            return res

        pick_scales(0, offs_t, "y_scales")
        pick_scales(1, two_t, "d_scales")
        y_words = keep.tile([P, N], U32, name="y_words", align_bytes=64)
        pick_words(0, offs_t, y_words[:])
        deal(deal_w1, raw_w1, deal_s1, raw_s1)
        y_ps = product(0)
        db_words = keep.tile([P, 2, N], U32, name="db_words", tag="staged_w1", align_bytes=64)
        pick_words(1, two_t, db_words[:, 0, :])
        pick_words(2, three_t, db_words[:, 1, :])
        pick_scales(2, three_t, "staged_s1")
        deal(deal_w23, raw_w23, deal_s23, raw_s23)
        d_ps = product(1)
        d_w = [keep.tile([P, 2 * N], F32, name="d_w%d" % t, align_bytes=64) for t in range(PACK)]
        for t in range(PACK):
            nc.scalar.activation(h_w[t][:, :N], y_ps[t][:], ACT.Copy, scale=ga_half[:, t : t + 1])
            nc.scalar.activation(d_w[t][:, N:], y_ps[t][:], ACT.Copy, scale=ga_abs[:, t : t + 1])
            nc.scalar.activation(d_w[t][:, :N], d_ps[t][:], ACT.Copy, scale=ga_abs[:, t : t + 1])
        b_ps = product(2)

        b4 = keep.tile([P, PACK, N], F32, name="b4", align_bytes=64)
        l_w = [keep.tile([P, 2 * N], F32, name="l_w%d" % t, align_bytes=64) for t in range(PACK)]
        r4 = keep.tile([P, PACK, N], F32, name="r4", align_bytes=64)
        for t in range(PACK):
            nc.scalar.activation(l_w[t][:, N:], b_ps[t][:], ACT.Abs)
            nc.scalar.activation(b4[:, t, :], b_ps[t][:], ACT.Copy, scale=gb_signed[:, t : t + 1])
        for t in range(PACK):
            nc.scalar.activation(l_w[t][:, :N], l_w[t][:, N:], ACT.Ln, bias=0.5)
        for t in range(PACK):
            nc.scalar.activation(r4[:, t, :], l_w[t][:].indirect(n4_t[:]), ACT.Exp, scale=-1.0)

        a4 = keep.tile([P, PACK, N], F32, name="a4", tag="staged_w23", align_bytes=64)
        g2 = keep.tile([P, PACK, N], F32, name="g2", align_bytes=64)
        g3 = keep.tile([P, PACK, N], BF16, name="g3", align_bytes=64)
        for t in range(PACK):
            nc.vector.tensor_tensor(a4[:, t, :], h_w[t][:].indirect(n1_t[:]), d_w[t][:, N:], ALU.add)
            nc.vector.tensor_copy(g2[:, t, :], d_w[t][:].indirect(n2_t[:]))
            nc.vector.tensor_copy(g3[:, t, :], d_w[t][:].indirect(n3_t[:]))

        low = keep.tile([P, PACK, N], BF16, name="low", align_bytes=64)
        z_p = keep.tile([P, PACK, N], BF16, name="z_p", align_bytes=64)
        nc.vector.tensor_tensor(low[:], a4[:], g2[:], ALU.min)
        nc.vector.tensor_tensor(z_p[:], low[:], g3[:], ALU.max)
        z_b = [keep.tile([P, 2 * P * PACK], BF16, name="z_b%d" % u, align_bytes=64) for u in range(2)]
        for u in range(2):
            nc.scalar.copy(
                z_b[u][:].rearrange("p (e m t) -> p e m t", e=2, t=PACK),
                z_p[:].rearrange("p t (m r) -> p r m t", r=PACK)[:, 2 * u : 2 * u + 2],
            )
        z2_b = keep.tile([P, N * PACK], BF16, name="z2_b", align_bytes=64)
        z2_w = keep.tile([P, N], U32, name="z2_w", align_bytes=64)
        z2_s = keep.tile([P, N], U8, name="z2_s", align_bytes=64)
        nc.vector.tensor_tensor(
            z2_b[:].rearrange("p (c i t) -> p c t i", i=2, t=PACK),
            b4[:].rearrange("p t (c i) -> p c t i", i=2),
            r4[:].rearrange("p t (c i) -> p c t i", i=2),
            ALU.mult,
        )
        z_w = [keep.tile([P, 2 * P], U32, name="z_w%d" % u, align_bytes=64) for u in range(2)]
        z_s = [keep.tile([P, 2 * P], U8, name="z_s%d" % u, align_bytes=64) for u in range(2)]

        s_w = h_w[: PACK - 1] + [keep.tile([P, N], F32, name="s_last", align_bytes=64)]

        def quantize_first(u):
            nc.vector.quantize_mx(out=z_w[u][:].bitcast(FP8X4), scales=z_s[u][:], in_=z_b[u][:])

        def score_bank(t, c0, width):
            bank = psum.tile([P, width], F32, name="bank")
            rows = slice(t % 2 * P, (t % 2 + 1) * P)
            nc.tensor.matmul_mx(
                out=bank[:], lhsT=z_w[t // 2][:, rows].bitcast(FP8X4), lhsT_scale=z_s[t // 2][:, rows],
                rhs=z2_w[:, c0 : c0 + width].bitcast(FP8X4), rhs_scale=z2_s[:, c0 : c0 + width], start=True, stop=True,
            )
            return bank

        quantize_first(0)
        nc.vector.quantize_mx(out=z2_w[:].bitcast(FP8X4), scales=z2_s[:], in_=z2_b[:])
        quantize_first(1)
        left, right = score_bank(0, 0, HALF), score_bank(0, HALF, HALF)
        nc.scalar.activation(s_w[0][:, :HALF], left[:], ACT.Copy, scale=0.0625)
        nc.vector.tensor_scalar(s_w[0][:, HALF:N], right[:], 0.0625, None, ALU.mult)
        for t in range(1, PACK):
            nc.scalar.activation(s_w[t][:, :N], score_bank(t, 0, N)[:], ACT.Copy, scale=0.0625)

        out_rows = out_0.rearrange("(p t) v -> p t v", t=PACK)
        out_words = out_1[0].rearrange("p n t -> p (n t)").bitcast(I32)
        o_w = keep.tile([P, N], U32, name="o_w", align_bytes=64)
        o_s = keep.tile([P, N], U8, name="o_s", align_bytes=64)

        def finish(c0, width, o_b):
            nc.vector.quantize_mx(out=o_w[:, c0 : c0 + width].bitcast(FP8X4), scales=o_s[:, c0 : c0 + width], in_=o_b[:])
            nc.sync.dma_start(out_words[:, c0 : c0 + width], o_w[:, c0 : c0 + width].bitcast(I32))

        g6 = keep.tile([P, PACK, N], F32, name="g6", align_bytes=64)
        o4 = keep.tile([P, PACK, N], F32, name="o4", align_bytes=64)

        def fetch(t, c0, width):
            nc.vector.tensor_copy(g6[:, t, c0 : c0 + width], s_w[t][:].indirect(entries(n6_t, c0, width)))

        def gap(t, c0, width):
            cols = slice(c0, c0 + width)
            nc.vector.tensor_tensor(o4[:, t, cols], s_w[t][:].indirect(entries(n5_t, c0, width)), g6[:, t, cols], ALU.subtract)
            nc.sync.dma_start(out_rows[:, t, cols], o4[:, t, cols])

        def round_pair(copy, first, c0, width, o_b):
            copy(
                o_b[:].rearrange("p (c t) -> p c t", t=PACK)[:, :, first : first + 2],
                o4[:, first : first + 2, c0 : c0 + width].rearrange("p t c -> p c t"),
            )

        rounded = [
            (c0, width, keep.tile([P, width * PACK], BF16, name="o_b%d" % c0, align_bytes=64))
            for c0, width in OUT_PIECES
        ]
        last = PACK - 1
        fetch(0, 0, N)
        fetch(1, 0, N)
        gap(0, 0, N)
        gap(1, 0, N)
        for piece in rounded:
            round_pair(nc.scalar.copy, 0, *piece)
        fetch(2, 0, N)
        fetch(last, 0, HALF)
        fetch(last, HALF, HALF)
        gap(2, 0, N)
        for piece in rounded:
            gap(last, piece[0], piece[1])
            round_pair(nc.vector.tensor_copy if piece[0] == OUT_PIECES[-1][0] else nc.scalar.copy, 2, *piece)
        for piece in rounded:
            finish(*piece)
        for q in range(4):
            queue = nc.scalar if q % 2 else nc.sync
            queue.dma_start(out_2[0, 4 * q : 4 * q + 4, :].bitcast(I32), o_s[32 * q : 32 * q + 4, :].bitcast(I32))
